import numpy as np
import ml_dtypes


def mxq(x, axis, fmt="e4m3"):
    dtype, down = {"e4m3": (ml_dtypes.float8_e4m3fn, 7), "e5m2": (ml_dtypes.float8_e5m2, 14)}[fmt]
    v = np.moveaxis(np.asarray(x, np.float32).astype(ml_dtypes.bfloat16).astype(np.float64), axis, -1)
    blocks = v.reshape(v.shape[:-1] + (-1, 32))
    amax = np.abs(blocks).max(-1, keepdims=True)
    byte = np.maximum(np.where(amax > 0, np.frexp(amax)[1] - 1 + 127, 0) - down, 1)
    scale = np.exp2(byte - 127.0)
    codes = (blocks / scale).astype(np.float32).astype(dtype).astype(np.float64)
    return np.moveaxis((codes * scale).reshape(v.shape), -1, axis)


WIDE = False


def mx_kscale(k):
    if not WIDE:
        return np.ones(k)
    levels = np.array([10, -10, 5, -5, 0])
    if k % 512:
        return np.exp2(np.random.permutation(np.resize(levels, k // 32))).repeat(32)
    a = np.empty((k // 512, 16))
    for p in range(k // 512):
        a[p, :8] = np.random.permutation(np.resize(levels, 8))
        for g in range(8):
            far = levels[np.abs(levels - a[p, g]) >= 10]
            a[p, g + 8] = far[np.random.randint(len(far))]
    return np.exp2(a.ravel()).repeat(32)


def f64(x):
    return np.asarray(x).astype(np.float64)


def striped(idx):
    return np.tile(np.asarray(idx).reshape(-1, 16).T, (8, 1)).astype(np.uint16)


def unstriped(offs):
    return offs[:16].T.reshape(-1).astype(np.int64)


def rot(x):
    y = x.reshape(-1, 2, x.shape[1])
    return np.stack([-y[:, 1], y[:, 0]], axis=1).reshape(x.shape)


D, T, I, U, V, Q = 512, 1024, 256, 512, 1024, 256


def setup_inputs():
    n = np.random.standard_normal
    idx = np.random.permutation(T)[:I]
    idx2 = np.random.permutation(T)[:I]
    idx3 = np.random.randint(0, U, I)
    idx4 = np.random.permutation(V)[:Q]
    fd = mx_kscale(D)
    return {
        "query": (n((D, V)) * 0.7 / np.sqrt(D) * fd[:, None]).astype(np.float32),
        "keys": (n((D, T)) / fd[:, None]).astype(np.float32),
        "cosn": (np.repeat(np.round(np.cos(np.arange(D // 2)[:, None] * 0.11 + np.arange(U)[None] * 0.37) * 64) / 64, 2, axis=0)).astype(np.float32),
        "sinn": (np.repeat(np.round(np.sin(np.arange(D // 2)[:, None] * 0.11 + np.arange(U)[None] * 0.37) * 64) / 64, 2, axis=0)).astype(np.float32),
        "kept": (n((D, T)) * 0.7 / fd[:, None]).astype(np.float32),
        "offs": striped(idx),
        "offs2": striped(idx2),
        "offs3": striped(idx3),
        "offs4": striped(idx4),
    }


def reference(query, keys, cosn, sinn, kept, offs, offs2, offs3, offs4):
    idx = unstriped(offs)
    idx2 = unstriped(offs2)
    idx3 = unstriped(offs3)
    idx4 = unstriped(offs4)
    kr = rot(f64(keys)[:, idx])
    kt = f64(keys)[:, idx] * f64(cosn)[:, idx3] + kr * f64(sinn)[:, idx3]
    kf = np.zeros((D, T))
    kf[:, idx2] = kt
    kn = kf + f64(kept)
    queryidx4q = mxq(f64(query)[:, idx4], 0, "e4m3")
    knq = mxq(kn, 0, "e4m3")
    a = queryidx4q.T @ knq
    p = np.exp(a - np.max(a, axis=1, keepdims=True))
    y = p / np.sum(p, axis=1, keepdims=True) * 512.0
    return y

@@ -1,0 +1,219 @@
+from contextlib import ExitStack
+
+import concourse.mybir as mybir
+from concourse.masks import make_identity
+
+D, T, I, U, V, Q = 512, 1024, 256, 512, 1024, 256
+FLOPS = 2 * D * Q * T
+BYTES = 4 * (3 * D * T + D * U + Q * T) + 4 * 128 * 16 * 2
+
+F32 = mybir.dt.float32
+BF16 = mybir.dt.bfloat16
+U32 = mybir.dt.uint32
+U16 = mybir.dt.uint16
+U8 = mybir.dt.uint8
+FP8X4 = mybir.dt.float8_e4m3fn_x4
+ALU = mybir.AluOpType
+ACT = mybir.ActivationFunctionType
+AXIS = mybir.AxisListType
+
+P = 128
+PACK = 4
+QUARTER = T // 4
+HALF = T // 2
+
+
+def tile_attend_turnedkeys_kernel(tc, query, keys, cosn, sinn, kept, offs, offs2, offs3, offs4, out):
+    nc = tc.nc
+    with ExitStack() as ctx:
+        lists = ctx.enter_context(tc.tile_pool(name="lists", bufs=1))
+        sb = ctx.enter_context(tc.tile_pool(name="sb", bufs=1))
+        ps = ctx.enter_context(tc.psum_pool(name="ps", bufs=1))
+
+        def plane(src, j):
+            return src.rearrange("(p j) c -> p j c", j=PACK)[:, j, :]
+
+        def load_list(src, name):
+            t = lists.tile([P, I // 16], U16, name=name)
+            nc.sync.dma_start(t[:], src)
+            return t
+
+        def load_plane(src, j, name):
+            t = sb.tile([P, src.shape[1]], F32, name=name, align_bytes=64)
+            nc.sync.dma_start(t[:], plane(src, j))
+            return t
+
+        key_p, cos_p, sin_p, qry_p, kept_p = {}, {}, {}, {}, {}
+        key_p[0] = load_plane(keys, 0, "key0")
+        key_list = load_list(offs, "key_list")
+        key_p[1] = load_plane(keys, 1, "key1")
+        dist_list = load_list(offs3, "dist_list")
+        cos_p[0] = load_plane(cosn, 0, "cos0")
+        sin_p[0] = load_plane(sinn, 0, "sin0")
+        place_list = load_list(offs2, "place_list")
+        qry_list = load_list(offs4, "qry_list")
+        qry_p[0] = load_plane(query, 0, "qry0")
+        kept_p[0] = load_plane(kept, 0, "kept0")
+        kept_p[1] = load_plane(kept, 1, "kept1")
+        key_p[2] = load_plane(keys, 2, "key2")
+        key_p[3] = load_plane(keys, 3, "key3")
+        cos_p[1] = load_plane(cosn, 2, "cos1")
+        sin_p[1] = load_plane(sinn, 2, "sin1")
+        qry_p[1] = load_plane(query, 1, "qry1")
+        kept_p[2] = load_plane(kept, 2, "kept2")
+        kept_p[3] = load_plane(kept, 3, "kept3")
+        qry_p[2] = load_plane(query, 2, "qry2")
+        qry_p[3] = load_plane(query, 3, "qry3")
+
+        warm_in = sb.tile([P, 1], F32, name="warm_in")
+        warm_out = sb.tile([P, 1], F32, name="warm_out")
+        nc.vector.memset(warm_in[:], 0.0)
+        nc.scalar.activation(warm_out[:], warm_in[:], ACT.Exp)
+
+        ident = sb.tile([P, P], F32, name="ident", align_bytes=64)
+        make_identity(nc, ident[:])
+
+        kf = [sb.tile([P, T], F32, name="kf%d" % j, align_bytes=64) for j in range(PACK)]
+        for j in range(PACK):
+            nc.vector.memset(kf[j][:], 0.0)
+
+        q_in = sb.tile([P, Q, PACK], BF16, name="q_in", align_bytes=64)
+
+        def query_on_scalar(j):
+            cast = sb.tile([P, V], BF16, name="qcast%d" % j, align_bytes=64)
+            nc.scalar.activation(cast[:], qry_p[j][:], ACT.Copy)
+            nc.scalar.activation(q_in[:, :, j], cast[:].indirect(qry_list[:]), ACT.Copy)
+
+        def query_on_vector(j):
+            nc.vector.tensor_copy(q_in[:, :, j], qry_p[j][:].indirect(qry_list[:]))
+
+        def turn_and_place(u):
+            kg = sb.tile([P, 2, I], F32, name="kg%d" % u, align_bytes=64)
+            cg = sb.tile([P, I], F32, name="cg%d" % u, align_bytes=64)
+            sg = sb.tile([P, I], F32, name="sg%d" % u, align_bytes=64)
+            kc = sb.tile([P, 2, I], F32, name="kc%d" % u, align_bytes=64)
+            ks = sb.tile([P, 2, I], F32, name="ks%d" % u, align_bytes=64)
+            for e in range(2):
+                nc.vector.tensor_copy(kg[:, e, :], key_p[2 * u + e][:].indirect(key_list[:]))
+            nc.vector.tensor_copy(cg[:], cos_p[u][:].indirect(dist_list[:]))
+            nc.vector.tensor_tensor(kc[:], kg[:], cg[:].unsqueeze(1).to_broadcast([P, 2, I]), ALU.mult)
+            nc.vector.tensor_copy(sg[:], sin_p[u][:].indirect(dist_list[:]))
+            nc.vector.scalar_tensor_tensor(ks[:, 0, :], kg[:, 1, :], -1.0, sg[:], ALU.mult, ALU.mult)
+            nc.vector.tensor_tensor(ks[:, 1, :], kg[:, 0, :], sg[:], ALU.mult)
+            for e in range(2):
+                nc.vector.tensor_tensor(kf[2 * u + e][:].indirect(place_list[:]), kc[:, e, :], ks[:, e, :], ALU.add)
+
+        def sum_banks(u):
+            return [ps.tile([P, 2, 2, P], F32, name="sum%d_%d" % (u, g), tag="bank%d" % (4 * u + g)) for g in range(4)]
+
+        def turn_into(banks, src, e, start, stop):
+            for g in range(4):
+                for h in range(2):
+                    c0 = g * QUARTER + h * P
+                    nc.tensor.matmul(banks[g][:, h, e, :], src[:, c0 : c0 + P], ident[:], is_transpose=True,
+                                     start=(start and h == 0), stop=(stop and h == 1))
+
+        def round_out(bank, u, g, on_vector):
+            rounded = sb.tile([P, 2, P, 2], BF16, name="rounded%d_%d" % (u, g), align_bytes=64)
+            src = bank[:].rearrange("t h e p -> t h p e")
+            if on_vector:
+                nc.vector.tensor_copy(rounded[:], src)
+            else:
+                nc.scalar.copy(rounded[:], src)
+            return rounded
+
+        def turn_back(back, rounded, u):
+            words = rounded[:].rearrange("t h p e -> t (h p e)").bitcast(F32)
+            for h in range(2):
+                nc.tensor.transpose(back[:, u, h * P : (h + 1) * P], words[:, h * P : (h + 1) * P], ident[:])
+
+        turn_and_place(0)
+        query_on_scalar(0)
+        sums0 = sum_banks(0)
+        sums1 = sum_banks(1)
+        turn_into(sums0, kept_p[0], 0, True, False)
+        turn_into(sums0, kept_p[1], 1, False, False)
+        turn_into(sums0, kf[0], 0, False, False)
+        turn_into(sums0, kf[1], 1, False, True)
+        backs = []
+        for g in range(4):
+            rounded = round_out(sums0[g], 0, g, False)
+            back = ps.tile([P, 2, QUARTER], F32, name="back%d" % g, tag="bank%d" % g)
+            turn_back(back, rounded, 0)
+            backs.append(back)
+        turn_and_place(1)
+        query_on_scalar(1)
+        turn_into(sums1, kept_p[2], 0, True, False)
+        turn_into(sums1, kept_p[3], 1, False, False)
+        turn_into(sums1, kf[2], 0, False, False)
+        turn_into(sums1, kf[3], 1, False, True)
+        query_on_vector(2)
+        query_on_vector(3)
+        q_codes = sb.tile([P, Q], U32, name="q_codes", align_bytes=64)
+        q_scales = sb.tile([P, Q], U8, name="q_scales", align_bytes=64)
+        nc.vector.quantize_mx(q_codes[:].bitcast(FP8X4), q_scales[:], q_in[:].rearrange("p q j -> p (q j)"))
+
+        for g in range(4):
+            rounded = round_out(sums1[g], 1, g, g == 3)
+            turn_back(backs[g], rounded, 1)
+        scores = {}
+        for h in range(2):
+            for m in range(2):
+                scores[m, h] = ps.tile([P, HALF], F32, name="score%d_%d" % (m, h), tag="bank%d" % (4 + 2 * h + m))
+        k_in = []
+        for g in range(4):
+            words = sb.tile([P, QUARTER * PACK], BF16, name="k_in%d" % g, align_bytes=64)
+            dst = words[:].bitcast(F32).rearrange("p (t u) -> p t u", u=2)
+            src = backs[g][:].rearrange("p u t -> p t u")
+            if g == 1:
+                nc.vector.tensor_copy(dst, src)
+            else:
+                nc.scalar.copy(dst, src)
+            k_in.append(words)
+        for g in range(4):
+            k_codes = sb.tile([P, QUARTER], U32, name="k_codes%d" % g, align_bytes=64)
+            k_scales = sb.tile([P, QUARTER], U8, name="k_scales%d" % g, align_bytes=64)
+            nc.vector.quantize_mx(k_codes[:].bitcast(FP8X4), k_scales[:], k_in[g][:])
+            cols = slice((g % 2) * QUARTER, (g % 2 + 1) * QUARTER)
+            for m in range(2):
+                rows = slice(m * P, (m + 1) * P)
+                nc.tensor.matmul_mx(scores[m, g // 2][:, cols], lhsT=q_codes[:, rows].bitcast(FP8X4), lhsT_scale=q_scales[:, rows],
+                                    rhs=k_codes[:].bitcast(FP8X4), rhs_scale=k_scales[:], start=True, stop=True)
+
+        def column(name):
+            return sb.tile([P, 1], F32, name=name)
+
+        st = {}
+        for m in range(2):
+            neg0 = column("neg0_%d" % m)
+            sum0 = column("sum0_%d" % m)
+            p0 = sb.tile([P, HALF], F32, name="p0_%d" % m, align_bytes=64)
+            nc.vector.tensor_reduce(neg0[:], scores[m, 0][:], AXIS.X, ALU.max, negate=True)
+            nc.scalar.activation(p0[:], scores[m, 0][:], ACT.Exp, bias=neg0[:], accum_out=sum0[:])
+            st[m] = (neg0, sum0, p0)
+        st2 = {}
+        for m in range(2):
+            neg0, sum0, p0 = st[m]
+            neg = column("neg_%d" % m)
+            sum1 = column("sum1_%d" % m)
+            shrink = column("shrink_%d" % m)
+            shrink512 = column("shrink512_%d" % m)
+            flipped = sb.tile([P, HALF], F32, name="flipped_%d" % m, align_bytes=64)
+            p1 = sb.tile([P, HALF], F32, name="p1_%d" % m, align_bytes=64)
+            nc.vector.tensor_scalar(flipped[:], scores[m, 1][:], -1.0, neg0[:], ALU.mult, ALU.min, accum_out=neg[:])
+            nc.scalar.activation(shrink[:], neg0[:], ACT.Exp, bias=neg[:], scale=-1.0)
+            nc.scalar.activation(p1[:], flipped[:], ACT.Exp, bias=neg[:], scale=-1.0, accum_out=sum1[:])
+            st2[m] = (shrink, shrink512, sum1, p1)
+        for m in range(2):
+            neg0, sum0, p0 = st[m]
+            shrink, shrink512, sum1, p1 = st2[m]
+            total = column("total_%d" % m)
+            inv = column("inv_%d" % m)
+            y = sb.tile([P, T], F32, name="y_%d" % m, align_bytes=64)
+            nc.vector.tensor_scalar(shrink512[:], shrink[:], 512.0, None, ALU.mult)
+            nc.vector.scalar_tensor_tensor(total[:], sum0[:], shrink[:], sum1[:], ALU.mult, ALU.add)
+            nc.vector.reciprocal(inv[:], total[:])
+            nc.vector.tensor_scalar(y[:, :HALF], p0[:], inv[:], shrink512[:], ALU.mult, ALU.mult)
+            nc.sync.dma_start(out[m * P : (m + 1) * P, :HALF], y[:, :HALF])
+            nc.vector.tensor_scalar(y[:, HALF:], p1[:], inv[:], 512.0, ALU.mult, ALU.mult)
+            nc.sync.dma_start(out[m * P : (m + 1) * P, HALF:], y[:, HALF:])

@@ -41,27 +41,31 @@ def tile_attend_turnedkeys_kernel(tc, query, keys, cosn, sinn, kept, offs, offs2
         def load_plane(src, j, name):
             t = sb.tile([P, src.shape[1]], F32, name=name, align_bytes=64)
             nc.sync.dma_start(t[:], plane(src, j))
-            return t
+            return t[:]
+
+        def load_pair(src, u, name):
+            t = sb.tile([P, 2, src.shape[1]], F32, name=name, align_bytes=64)
+            nc.sync.dma_start(t[:], src.rearrange("(p j) c -> p j c", j=PACK)[:, 2 * u : 2 * u + 2, :])
+            return t[:, 0, :], t[:, 1, :]
 
         key_p, cos_p, sin_p, qry_p, kept_p = {}, {}, {}, {}, {}
-        key_p[0] = load_plane(keys, 0, "key0")
-        key_list = load_list(offs, "key_list")
-        key_p[1] = load_plane(keys, 1, "key1")
-        dist_list = load_list(offs3, "dist_list")
         cos_p[0] = load_plane(cosn, 0, "cos0")
+        dist_list = load_list(offs3, "dist_list")
         sin_p[0] = load_plane(sinn, 0, "sin0")
+        key_list = load_list(offs, "key_list")
+        key_p[0] = load_plane(keys, 0, "key0")
+        key_p[1] = load_plane(keys, 1, "key1")
         place_list = load_list(offs2, "place_list")
-        qry_list = load_list(offs4, "qry_list")
-        qry_p[0] = load_plane(query, 0, "qry0")
         kept_p[0] = load_plane(kept, 0, "kept0")
         kept_p[1] = load_plane(kept, 1, "kept1")
-        key_p[2] = load_plane(keys, 2, "key2")
-        key_p[3] = load_plane(keys, 3, "key3")
         cos_p[1] = load_plane(cosn, 2, "cos1")
         sin_p[1] = load_plane(sinn, 2, "sin1")
-        qry_p[1] = load_plane(query, 1, "qry1")
+        key_p[2], key_p[3] = load_pair(keys, 1, "key23")
         kept_p[2] = load_plane(kept, 2, "kept2")
+        qry_list = load_list(offs4, "qry_list")
+        qry_p[0] = load_plane(query, 0, "qry0")
         kept_p[3] = load_plane(kept, 3, "kept3")
+        qry_p[1] = load_plane(query, 1, "qry1")
         qry_p[2] = load_plane(query, 2, "qry2")
         qry_p[3] = load_plane(query, 3, "qry3")
 
@@ -75,33 +79,34 @@ def tile_attend_turnedkeys_kernel(tc, query, keys, cosn, sinn, kept, offs, offs2
 
         kf = [sb.tile([P, T], F32, name="kf%d" % j, align_bytes=64) for j in range(PACK)]
         for j in range(PACK):
-            nc.vector.memset(kf[j][:], 0.0)
+            nc.gpsimd.memset(kf[j][:], 0.0)
 
         q_in = sb.tile([P, Q, PACK], BF16, name="q_in", align_bytes=64)
 
         def query_on_scalar(j):
             cast = sb.tile([P, V], BF16, name="qcast%d" % j, align_bytes=64)
-            nc.scalar.activation(cast[:], qry_p[j][:], ACT.Copy)
+            nc.scalar.activation(cast[:], qry_p[j], ACT.Copy)
             nc.scalar.activation(q_in[:, :, j], cast[:].indirect(qry_list[:]), ACT.Copy)
 
         def query_on_vector(j):
-            nc.vector.tensor_copy(q_in[:, :, j], qry_p[j][:].indirect(qry_list[:]))
+            nc.vector.tensor_copy(q_in[:, :, j], qry_p[j].indirect(qry_list[:]))
 
         def turn_and_place(u):
-            kg = sb.tile([P, 2, I], F32, name="kg%d" % u, align_bytes=64)
-            cg = sb.tile([P, I], F32, name="cg%d" % u, align_bytes=64)
-            sg = sb.tile([P, I], F32, name="sg%d" % u, align_bytes=64)
-            kc = sb.tile([P, 2, I], F32, name="kc%d" % u, align_bytes=64)
-            ks = sb.tile([P, 2, I], F32, name="ks%d" % u, align_bytes=64)
-            for e in range(2):
-                nc.vector.tensor_copy(kg[:, e, :], key_p[2 * u + e][:].indirect(key_list[:]))
-            nc.vector.tensor_copy(cg[:], cos_p[u][:].indirect(dist_list[:]))
-            nc.vector.tensor_tensor(kc[:], kg[:], cg[:].unsqueeze(1).to_broadcast([P, 2, I]), ALU.mult)
-            nc.vector.tensor_copy(sg[:], sin_p[u][:].indirect(dist_list[:]))
-            nc.vector.scalar_tensor_tensor(ks[:, 0, :], kg[:, 1, :], -1.0, sg[:], ALU.mult, ALU.mult)
-            nc.vector.tensor_tensor(ks[:, 1, :], kg[:, 0, :], sg[:], ALU.mult)
-            for e in range(2):
-                nc.vector.tensor_tensor(kf[2 * u + e][:].indirect(place_list[:]), kc[:, e, :], ks[:, e, :], ALU.add)
+            even = sb.tile([P, I], F32, name="even%d" % u, align_bytes=64)
+            odd = sb.tile([P, I], F32, name="odd%d" % u, align_bytes=64)
+            cs = sb.tile([P, 2, I], F32, name="cs%d" % u, align_bytes=64)
+            even_cs = sb.tile([P, 2, I], F32, name="even_cs%d" % u, align_bytes=64)
+            odd_c = sb.tile([P, I], F32, name="odd_c%d" % u, align_bytes=64)
+            odd_s = sb.tile([P, I], F32, name="odd_s%d" % u, align_bytes=64)
+            nc.vector.tensor_copy(cs[:, 0, :], cos_p[u].indirect(dist_list[:]))
+            nc.vector.tensor_copy(cs[:, 1, :], sin_p[u].indirect(dist_list[:]))
+            nc.vector.tensor_copy(even[:], key_p[2 * u].indirect(key_list[:]))
+            nc.vector.tensor_copy(odd[:], key_p[2 * u + 1].indirect(key_list[:]))
+            nc.vector.tensor_tensor(even_cs[:], cs[:], even[:].unsqueeze(1).to_broadcast([P, 2, I]), ALU.mult)
+            nc.vector.scalar_tensor_tensor(odd_s[:], odd[:], -1.0, cs[:, 1, :], ALU.mult, ALU.mult)
+            nc.vector.tensor_tensor(odd_c[:], odd[:], cs[:, 0, :], ALU.mult)
+            nc.vector.tensor_tensor(kf[2 * u][:].indirect(place_list[:]), even_cs[:, 0, :], odd_s[:], ALU.add)
+            nc.vector.tensor_tensor(kf[2 * u + 1][:].indirect(place_list[:]), odd_c[:], even_cs[:, 1, :], ALU.add)
 
         def sum_banks(u):
             return [ps.tile([P, 2, 2, P], F32, name="sum%d_%d" % (u, g), tag="bank%d" % (4 * u + g)) for g in range(4)]
@@ -128,7 +133,6 @@ def tile_attend_turnedkeys_kernel(tc, query, keys, cosn, sinn, kept, offs, offs2
                 nc.tensor.transpose(back[:, u, h * P : (h + 1) * P], words[:, h * P : (h + 1) * P], ident[:])
 
         turn_and_place(0)
-        query_on_scalar(0)
         sums0 = sum_banks(0)
         sums1 = sum_banks(1)
         turn_into(sums0, kept_p[0], 0, True, False)
@@ -142,20 +146,20 @@ def tile_attend_turnedkeys_kernel(tc, query, keys, cosn, sinn, kept, offs, offs2
             turn_back(back, rounded, 0)
             backs.append(back)
         turn_and_place(1)
+        query_on_scalar(0)
         query_on_scalar(1)
         turn_into(sums1, kept_p[2], 0, True, False)
         turn_into(sums1, kept_p[3], 1, False, False)
         turn_into(sums1, kf[2], 0, False, False)
         turn_into(sums1, kf[3], 1, False, True)
         query_on_vector(2)
+        for g in range(3):
+            turn_back(backs[g], round_out(sums1[g], 1, g, g == 0), 1)
         query_on_vector(3)
+        turn_back(backs[3], round_out(sums1[3], 1, 3, True), 1)
         q_codes = sb.tile([P, Q], U32, name="q_codes", align_bytes=64)
         q_scales = sb.tile([P, Q], U8, name="q_scales", align_bytes=64)
         nc.vector.quantize_mx(q_codes[:].bitcast(FP8X4), q_scales[:], q_in[:].rearrange("p q j -> p (q j)"))
-
-        for g in range(4):
-            rounded = round_out(sums1[g], 1, g, g == 3)
-            turn_back(backs[g], rounded, 1)
         scores = {}
         for h in range(2):
             for m in range(2):
@@ -165,10 +169,7 @@ def tile_attend_turnedkeys_kernel(tc, query, keys, cosn, sinn, kept, offs, offs2
             words = sb.tile([P, QUARTER * PACK], BF16, name="k_in%d" % g, align_bytes=64)
             dst = words[:].bitcast(F32).rearrange("p (t u) -> p t u", u=2)
             src = backs[g][:].rearrange("p u t -> p t u")
-            if g == 1:
-                nc.vector.tensor_copy(dst, src)
-            else:
-                nc.scalar.copy(dst, src)
+            nc.scalar.copy(dst, src)
             k_in.append(words)
         for g in range(4):
             k_codes = sb.tile([P, QUARTER], U32, name="k_codes%d" % g, align_bytes=64)
@@ -180,40 +181,41 @@ def tile_attend_turnedkeys_kernel(tc, query, keys, cosn, sinn, kept, offs, offs2
                 nc.tensor.matmul_mx(scores[m, g // 2][:, cols], lhsT=q_codes[:, rows].bitcast(FP8X4), lhsT_scale=q_scales[:, rows],
                                     rhs=k_codes[:].bitcast(FP8X4), rhs_scale=k_scales[:], start=True, stop=True)
 
-        def column(name):
-            return sb.tile([P, 1], F32, name=name)
-
-        st = {}
+        negs, sums, probs = [], [], []
         for m in range(2):
-            neg0 = column("neg0_%d" % m)
-            sum0 = column("sum0_%d" % m)
-            p0 = sb.tile([P, HALF], F32, name="p0_%d" % m, align_bytes=64)
-            nc.vector.tensor_reduce(neg0[:], scores[m, 0][:], AXIS.X, ALU.max, negate=True)
-            nc.scalar.activation(p0[:], scores[m, 0][:], ACT.Exp, bias=neg0[:], accum_out=sum0[:])
-            st[m] = (neg0, sum0, p0)
-        st2 = {}
+            negs.append(sb.tile([P, 2], F32, name="negs%d" % m))
+            sums.append(sb.tile([P, 2], F32, name="sums%d" % m))
+            probs.append(sb.tile([P, T], F32, name="probs%d" % m, align_bytes=64))
+            nc.vector.tensor_reduce(negs[m][:, 0:1], scores[m, 0][:], AXIS.X, ALU.max, negate=True)
+            nc.scalar.activation(probs[m][:, :HALF], scores[m, 0][:], ACT.Exp, bias=negs[m][:, 0:1], accum_out=sums[m][:, 0:1])
+        shrinks = []
         for m in range(2):
-            neg0, sum0, p0 = st[m]
-            neg = column("neg_%d" % m)
-            sum1 = column("sum1_%d" % m)
-            shrink = column("shrink_%d" % m)
-            shrink512 = column("shrink512_%d" % m)
-            flipped = sb.tile([P, HALF], F32, name="flipped_%d" % m, align_bytes=64)
-            p1 = sb.tile([P, HALF], F32, name="p1_%d" % m, align_bytes=64)
-            nc.vector.tensor_scalar(flipped[:], scores[m, 1][:], -1.0, neg0[:], ALU.mult, ALU.min, accum_out=neg[:])
-            nc.scalar.activation(shrink[:], neg0[:], ACT.Exp, bias=neg[:], scale=-1.0)
-            nc.scalar.activation(p1[:], flipped[:], ACT.Exp, bias=neg[:], scale=-1.0, accum_out=sum1[:])
-            st2[m] = (shrink, shrink512, sum1, p1)
-        for m in range(2):
-            neg0, sum0, p0 = st[m]
-            shrink, shrink512, sum1, p1 = st2[m]
-            total = column("total_%d" % m)
-            inv = column("inv_%d" % m)
-            y = sb.tile([P, T], F32, name="y_%d" % m, align_bytes=64)
-            nc.vector.tensor_scalar(shrink512[:], shrink[:], 512.0, None, ALU.mult)
-            nc.vector.scalar_tensor_tensor(total[:], sum0[:], shrink[:], sum1[:], ALU.mult, ALU.add)
+            flipped = sb.tile([P, HALF], F32, name="flipped%d" % m, align_bytes=64)
+            shrinks.append(sb.tile([P, 2], F32, name="shrink%d" % m))
+            nc.vector.tensor_scalar(flipped[:], scores[m, 1][:], -1.0, negs[m][:, 0:1], ALU.mult, ALU.min, accum_out=negs[m][:, 1:2])
+            nc.scalar.activation(shrinks[m][:], negs[m][:], ACT.Exp, bias=negs[m][:, 1:2], scale=-1.0)
+            nc.scalar.activation(probs[m][:, HALF:], flipped[:], ACT.Exp, bias=negs[m][:, 1:2], scale=-1.0, accum_out=sums[m][:, 1:2])
+        def inverse_total(m):
+            terms = sb.tile([P, 2], F32, name="terms%d" % m)
+            total = sb.tile([P, 1], F32, name="total%d" % m)
+            inv = sb.tile([P, 1], F32, name="inv%d" % m)
+            nc.vector.scalar_tensor_tensor(terms[:], sums[m][:], 1.0 / 512.0, shrinks[m][:], ALU.mult, ALU.mult, accum_out=total[:])
             nc.vector.reciprocal(inv[:], total[:])
-            nc.vector.tensor_scalar(y[:, :HALF], p0[:], inv[:], shrink512[:], ALU.mult, ALU.mult)
-            nc.sync.dma_start(out[m * P : (m + 1) * P, :HALF], y[:, :HALF])
-            nc.vector.tensor_scalar(y[:, HALF:], p1[:], inv[:], 512.0, ALU.mult, ALU.mult)
-            nc.sync.dma_start(out[m * P : (m + 1) * P, HALF:], y[:, HALF:])
+            return inv
+
+        def store(m, h, y):
+            nc.sync.dma_start(out[m * P : (m + 1) * P, h * HALF : (h + 1) * HALF], y[:])
+
+        ys = {(m, h): sb.tile([P, HALF], F32, name="y%d_%d" % (m, h), align_bytes=64) for m in range(2) for h in range(2)}
+        inv = inverse_total(0)
+        factor = sb.tile([P, 1], F32, name="factor")
+        nc.vector.tensor_tensor(factor[:], inv[:], shrinks[0][:, 0:1], ALU.mult)
+        nc.vector.tensor_scalar(ys[0, 1][:], probs[0][:, HALF:], inv[:], None, ALU.mult)
+        store(0, 1, ys[0, 1])
+        nc.scalar.activation(ys[0, 0][:], probs[0][:, :HALF], ACT.Copy, scale=factor[:])
+        store(0, 0, ys[0, 0])
+        inv = inverse_total(1)
+        nc.vector.tensor_scalar(ys[1, 0][:], probs[1][:, :HALF], inv[:], shrinks[1][:, 0:1], ALU.mult, ALU.mult)
+        store(1, 0, ys[1, 0])
+        nc.vector.tensor_scalar(ys[1, 1][:], probs[1][:, HALF:], inv[:], None, ALU.mult)
+        store(1, 1, ys[1, 1])

@@ -18,9 +18,11 @@ ACT = mybir.ActivationFunctionType
 AXIS = mybir.AxisListType
 
 P = 128
-PACK = 4
-QUARTER = T // 4
+PLANES = 4
+QUARTERS = 4
+QUARTER = T // QUARTERS
 HALF = T // 2
+OUT_SCALE = 512.0
 
 
 def tile_attend_turnedkeys_kernel(tc, query, keys, cosn, sinn, kept, offs, offs2, offs3, offs4, out):
@@ -30,148 +32,141 @@ def tile_attend_turnedkeys_kernel(tc, query, keys, cosn, sinn, kept, offs, offs2
         sb = ctx.enter_context(tc.tile_pool(name="sb", bufs=1))
         ps = ctx.enter_context(tc.psum_pool(name="ps", bufs=1))
 
-        def plane(src, j):
-            return src.rearrange("(p j) c -> p j c", j=PACK)[:, j, :]
-
         def load_list(src, name):
-            t = lists.tile([P, I // 16], U16, name=name)
-            nc.sync.dma_start(t[:], src)
-            return t
+            tile = lists.tile([P, I // 16], U16, name=name)
+            nc.sync.dma_start(tile[:], src)
+            return tile
 
         def load_plane(src, j, name):
-            t = sb.tile([P, src.shape[1]], F32, name=name, align_bytes=64)
-            nc.sync.dma_start(t[:], plane(src, j))
-            return t[:]
+            tile = sb.tile([P, src.shape[1]], F32, name=name, align_bytes=64)
+            nc.sync.dma_start(tile[:], src.rearrange("(p j) c -> p j c", j=PLANES)[:, j, :])
+            return tile[:]
 
         def load_pair(src, u, name):
-            t = sb.tile([P, 2, src.shape[1]], F32, name=name, align_bytes=64)
-            nc.sync.dma_start(t[:], src.rearrange("(p j) c -> p j c", j=PACK)[:, 2 * u : 2 * u + 2, :])
-            return t[:, 0, :], t[:, 1, :]
+            tile = sb.tile([P, 2, src.shape[1]], F32, name=name, align_bytes=64)
+            nc.sync.dma_start(tile[:], src.rearrange("(p j) c -> p j c", j=PLANES)[:, 2 * u : 2 * u + 2, :])
+            return tile[:, 0, :], tile[:, 1, :]
 
-        key_p, cos_p, sin_p, qry_p, kept_p = {}, {}, {}, {}, {}
-        cos_p[0] = load_plane(cosn, 0, "cos0")
-        dist_list = load_list(offs3, "dist_list")
-        sin_p[0] = load_plane(sinn, 0, "sin0")
+        key_plane, cos_plane, sin_plane, query_plane, kept_plane = {}, {}, {}, {}, {}
+        cos_plane[0] = load_plane(cosn, 0, "cos0")
+        distance_list = load_list(offs3, "distance_list")
+        sin_plane[0] = load_plane(sinn, 0, "sin0")
         key_list = load_list(offs, "key_list")
-        key_p[0] = load_plane(keys, 0, "key0")
-        key_p[1] = load_plane(keys, 1, "key1")
+        key_plane[0] = load_plane(keys, 0, "key0")
+        key_plane[1] = load_plane(keys, 1, "key1")
         place_list = load_list(offs2, "place_list")
-        kept_p[0] = load_plane(kept, 0, "kept0")
-        kept_p[1] = load_plane(kept, 1, "kept1")
-        cos_p[1] = load_plane(cosn, 2, "cos1")
-        sin_p[1] = load_plane(sinn, 2, "sin1")
-        key_p[2], key_p[3] = load_pair(keys, 1, "key23")
-        kept_p[2] = load_plane(kept, 2, "kept2")
-        qry_list = load_list(offs4, "qry_list")
-        qry_p[0] = load_plane(query, 0, "qry0")
-        kept_p[3] = load_plane(kept, 3, "kept3")
-        qry_p[1] = load_plane(query, 1, "qry1")
-        qry_p[2] = load_plane(query, 2, "qry2")
-        qry_p[3] = load_plane(query, 3, "qry3")
-
-        warm_in = sb.tile([P, 1], F32, name="warm_in")
-        warm_out = sb.tile([P, 1], F32, name="warm_out")
-        nc.vector.memset(warm_in[:], 0.0)
-        nc.scalar.activation(warm_out[:], warm_in[:], ACT.Exp)
+        kept_plane[0] = load_plane(kept, 0, "kept0")
+        kept_plane[1] = load_plane(kept, 1, "kept1")
+        cos_plane[1] = load_plane(cosn, 2, "cos1")
+        sin_plane[1] = load_plane(sinn, 2, "sin1")
+        key_plane[2], key_plane[3] = load_pair(keys, 1, "key23")
+        kept_plane[2] = load_plane(kept, 2, "kept2")
+        query_list = load_list(offs4, "query_list")
+        query_plane[0] = load_plane(query, 0, "query0")
+        kept_plane[3] = load_plane(kept, 3, "kept3")
+        query_plane[1] = load_plane(query, 1, "query1")
+        query_plane[2] = load_plane(query, 2, "query2")
+        query_plane[3] = load_plane(query, 3, "query3")
 
         ident = sb.tile([P, P], F32, name="ident", align_bytes=64)
         make_identity(nc, ident[:])
 
-        kf = [sb.tile([P, T], F32, name="kf%d" % j, align_bytes=64) for j in range(PACK)]
-        for j in range(PACK):
+        kf = [sb.tile([P, T], F32, name="kf%d" % j, align_bytes=64) for j in range(PLANES)]
+        for j in range(PLANES):
             nc.gpsimd.memset(kf[j][:], 0.0)
 
-        q_in = sb.tile([P, Q, PACK], BF16, name="q_in", align_bytes=64)
+        q_in = sb.tile([P, Q, PLANES], BF16, name="q_in", align_bytes=64)
 
-        def query_on_scalar(j):
-            cast = sb.tile([P, V], BF16, name="qcast%d" % j, align_bytes=64)
-            nc.scalar.activation(cast[:], qry_p[j], ACT.Copy)
-            nc.scalar.activation(q_in[:, :, j], cast[:].indirect(qry_list[:]), ACT.Copy)
+        def gather_query_on_scalar(j):
+            cast = sb.tile([P, V], BF16, name="query_bf16_%d" % j, align_bytes=64)
+            nc.scalar.activation(cast[:], query_plane[j], ACT.Copy)
+            nc.scalar.activation(q_in[:, :, j], cast[:].indirect(query_list[:]), ACT.Copy)
 
-        def query_on_vector(j):
-            nc.vector.tensor_copy(q_in[:, :, j], qry_p[j].indirect(qry_list[:]))
+        def gather_query_on_vector(j):
+            nc.vector.tensor_copy(q_in[:, :, j], query_plane[j].indirect(query_list[:]))
 
         def turn_and_place(u):
             even = sb.tile([P, I], F32, name="even%d" % u, align_bytes=64)
             odd = sb.tile([P, I], F32, name="odd%d" % u, align_bytes=64)
-            cs = sb.tile([P, 2, I], F32, name="cs%d" % u, align_bytes=64)
-            even_cs = sb.tile([P, 2, I], F32, name="even_cs%d" % u, align_bytes=64)
-            odd_c = sb.tile([P, I], F32, name="odd_c%d" % u, align_bytes=64)
-            odd_s = sb.tile([P, I], F32, name="odd_s%d" % u, align_bytes=64)
-            nc.vector.tensor_copy(cs[:, 0, :], cos_p[u].indirect(dist_list[:]))
-            nc.vector.tensor_copy(cs[:, 1, :], sin_p[u].indirect(dist_list[:]))
-            nc.vector.tensor_copy(even[:], key_p[2 * u].indirect(key_list[:]))
-            nc.vector.tensor_copy(odd[:], key_p[2 * u + 1].indirect(key_list[:]))
-            nc.vector.tensor_tensor(even_cs[:], cs[:], even[:].unsqueeze(1).to_broadcast([P, 2, I]), ALU.mult)
-            nc.vector.scalar_tensor_tensor(odd_s[:], odd[:], -1.0, cs[:, 1, :], ALU.mult, ALU.mult)
-            nc.vector.tensor_tensor(odd_c[:], odd[:], cs[:, 0, :], ALU.mult)
-            nc.vector.tensor_tensor(kf[2 * u][:].indirect(place_list[:]), even_cs[:, 0, :], odd_s[:], ALU.add)
-            nc.vector.tensor_tensor(kf[2 * u + 1][:].indirect(place_list[:]), odd_c[:], even_cs[:, 1, :], ALU.add)
+            cos_sin = sb.tile([P, 2, I], F32, name="cos_sin%d" % u, align_bytes=64)
+            even_cos_sin = sb.tile([P, 2, I], F32, name="even_cos_sin%d" % u, align_bytes=64)
+            odd_cos = sb.tile([P, I], F32, name="odd_cos%d" % u, align_bytes=64)
+            minus_odd_sin = sb.tile([P, I], F32, name="minus_odd_sin%d" % u, align_bytes=64)
+            nc.vector.tensor_copy(cos_sin[:, 0, :], cos_plane[u].indirect(distance_list[:]))
+            nc.vector.tensor_copy(cos_sin[:, 1, :], sin_plane[u].indirect(distance_list[:]))
+            nc.vector.tensor_copy(even[:], key_plane[2 * u].indirect(key_list[:]))
+            nc.vector.tensor_copy(odd[:], key_plane[2 * u + 1].indirect(key_list[:]))
+            nc.vector.tensor_tensor(even_cos_sin[:], cos_sin[:], even[:].unsqueeze(1).to_broadcast([P, 2, I]), ALU.mult)
+            nc.vector.scalar_tensor_tensor(minus_odd_sin[:], odd[:], -1.0, cos_sin[:, 1, :], ALU.mult, ALU.mult)
+            nc.vector.tensor_tensor(odd_cos[:], odd[:], cos_sin[:, 0, :], ALU.mult)
+            nc.vector.tensor_tensor(kf[2 * u][:].indirect(place_list[:]), even_cos_sin[:, 0, :], minus_odd_sin[:], ALU.add)
+            nc.vector.tensor_tensor(kf[2 * u + 1][:].indirect(place_list[:]), odd_cos[:], even_cos_sin[:, 1, :], ALU.add)
 
         def sum_banks(u):
-            return [ps.tile([P, 2, 2, P], F32, name="sum%d_%d" % (u, g), tag="bank%d" % (4 * u + g)) for g in range(4)]
+            return [
+                ps.tile([P, 2, 2, P], F32, name="sum%d_%d" % (u, g), tag="bank%d" % (QUARTERS * u + g))
+                for g in range(QUARTERS)
+            ]
 
-        def turn_into(banks, src, e, start, stop):
-            for g in range(4):
-                for h in range(2):
-                    c0 = g * QUARTER + h * P
-                    nc.tensor.matmul(banks[g][:, h, e, :], src[:, c0 : c0 + P], ident[:], is_transpose=True,
-                                     start=(start and h == 0), stop=(stop and h == 1))
+        def add_transposed(banks, plane, e, start, stop):
+            for g in range(QUARTERS):
+                for b in range(2):
+                    c0 = g * QUARTER + b * P
+                    nc.tensor.matmul(banks[g][:, b, e, :], plane[:, c0 : c0 + P], ident[:], is_transpose=True,
+                                     start=(start and b == 0), stop=(stop and b == 1))
 
-        def round_out(bank, u, g, on_vector):
+        def sum_pair(banks, u):
+            add_transposed(banks, kept_plane[2 * u], 0, True, False)
+            add_transposed(banks, kept_plane[2 * u + 1], 1, False, False)
+            add_transposed(banks, kf[2 * u], 0, False, False)
+            add_transposed(banks, kf[2 * u + 1], 1, False, True)
+
+        def round_pair(bank, u, g, copy):
             rounded = sb.tile([P, 2, P, 2], BF16, name="rounded%d_%d" % (u, g), align_bytes=64)
-            src = bank[:].rearrange("t h e p -> t h p e")
-            if on_vector:
-                nc.vector.tensor_copy(rounded[:], src)
-            else:
-                nc.scalar.copy(rounded[:], src)
+            copy(rounded[:], bank[:].rearrange("t b e p -> t b p e"))
             return rounded
 
         def turn_back(back, rounded, u):
-            words = rounded[:].rearrange("t h p e -> t (h p e)").bitcast(F32)
-            for h in range(2):
-                nc.tensor.transpose(back[:, u, h * P : (h + 1) * P], words[:, h * P : (h + 1) * P], ident[:])
+            words = rounded[:].rearrange("t b p e -> t (b p e)").bitcast(F32)
+            for b in range(2):
+                nc.tensor.transpose(back[:, u, b * P : (b + 1) * P], words[:, b * P : (b + 1) * P], ident[:])
 
         turn_and_place(0)
         sums0 = sum_banks(0)
         sums1 = sum_banks(1)
-        turn_into(sums0, kept_p[0], 0, True, False)
-        turn_into(sums0, kept_p[1], 1, False, False)
-        turn_into(sums0, kf[0], 0, False, False)
-        turn_into(sums0, kf[1], 1, False, True)
+        sum_pair(sums0, 0)
         backs = []
-        for g in range(4):
-            rounded = round_out(sums0[g], 0, g, False)
+        for g in range(QUARTERS):
+            rounded = round_pair(sums0[g], 0, g, nc.scalar.copy)
             back = ps.tile([P, 2, QUARTER], F32, name="back%d" % g, tag="bank%d" % g)
             turn_back(back, rounded, 0)
             backs.append(back)
+
         turn_and_place(1)
-        query_on_scalar(0)
-        query_on_scalar(1)
-        turn_into(sums1, kept_p[2], 0, True, False)
-        turn_into(sums1, kept_p[3], 1, False, False)
-        turn_into(sums1, kf[2], 0, False, False)
-        turn_into(sums1, kf[3], 1, False, True)
-        query_on_vector(2)
-        for g in range(3):
-            turn_back(backs[g], round_out(sums1[g], 1, g, g == 0), 1)
-        query_on_vector(3)
-        turn_back(backs[3], round_out(sums1[3], 1, 3, True), 1)
+        gather_query_on_scalar(0)
+        gather_query_on_scalar(1)
+        sum_pair(sums1, 1)
+
+        gather_query_on_vector(2)
+        for g, copy in enumerate((nc.vector.tensor_copy, nc.scalar.copy, nc.scalar.copy)):
+            turn_back(backs[g], round_pair(sums1[g], 1, g, copy), 1)
+        gather_query_on_vector(3)
+        turn_back(backs[3], round_pair(sums1[3], 1, 3, nc.vector.tensor_copy), 1)
         q_codes = sb.tile([P, Q], U32, name="q_codes", align_bytes=64)
         q_scales = sb.tile([P, Q], U8, name="q_scales", align_bytes=64)
         nc.vector.quantize_mx(q_codes[:].bitcast(FP8X4), q_scales[:], q_in[:].rearrange("p q j -> p (q j)"))
+
         scores = {}
         for h in range(2):
             for m in range(2):
-                scores[m, h] = ps.tile([P, HALF], F32, name="score%d_%d" % (m, h), tag="bank%d" % (4 + 2 * h + m))
+                scores[m, h] = ps.tile([P, HALF], F32, name="score%d_%d" % (m, h), tag="bank%d" % (QUARTERS + 2 * h + m))
+
         k_in = []
-        for g in range(4):
-            words = sb.tile([P, QUARTER * PACK], BF16, name="k_in%d" % g, align_bytes=64)
-            dst = words[:].bitcast(F32).rearrange("p (t u) -> p t u", u=2)
-            src = backs[g][:].rearrange("p u t -> p t u")
-            nc.scalar.copy(dst, src)
-            k_in.append(words)
-        for g in range(4):
+        for g in range(QUARTERS):
+            interleaved = sb.tile([P, QUARTER * PLANES], BF16, name="k_in%d" % g, align_bytes=64)
+            nc.scalar.copy(interleaved[:].bitcast(F32).rearrange("p (t u) -> p t u", u=2), backs[g][:].rearrange("p u t -> p t u"))
+            k_in.append(interleaved)
+        for g in range(QUARTERS):
             k_codes = sb.tile([P, QUARTER], U32, name="k_codes%d" % g, align_bytes=64)
             k_scales = sb.tile([P, QUARTER], U8, name="k_scales%d" % g, align_bytes=64)
             nc.vector.quantize_mx(k_codes[:].bitcast(FP8X4), k_scales[:], k_in[g][:])
@@ -181,41 +176,42 @@ def tile_attend_turnedkeys_kernel(tc, query, keys, cosn, sinn, kept, offs, offs2
                 nc.tensor.matmul_mx(scores[m, g // 2][:, cols], lhsT=q_codes[:, rows].bitcast(FP8X4), lhsT_scale=q_scales[:, rows],
                                     rhs=k_codes[:].bitcast(FP8X4), rhs_scale=k_scales[:], start=True, stop=True)
 
-        negs, sums, probs = [], [], []
+        minus_max, half_sums, probs = [], [], []
         for m in range(2):
-            negs.append(sb.tile([P, 2], F32, name="negs%d" % m))
-            sums.append(sb.tile([P, 2], F32, name="sums%d" % m))
+            minus_max.append(sb.tile([P, 2], F32, name="minus_max%d" % m))
+            half_sums.append(sb.tile([P, 2], F32, name="half_sums%d" % m))
             probs.append(sb.tile([P, T], F32, name="probs%d" % m, align_bytes=64))
-            nc.vector.tensor_reduce(negs[m][:, 0:1], scores[m, 0][:], AXIS.X, ALU.max, negate=True)
-            nc.scalar.activation(probs[m][:, :HALF], scores[m, 0][:], ACT.Exp, bias=negs[m][:, 0:1], accum_out=sums[m][:, 0:1])
-        shrinks = []
+            nc.vector.tensor_reduce(minus_max[m][:, 0:1], scores[m, 0][:], AXIS.X, ALU.max, negate=True)
+            nc.scalar.activation(probs[m][:, :HALF], scores[m, 0][:], ACT.Exp, bias=minus_max[m][:, 0:1], accum_out=half_sums[m][:, 0:1])
+        shrink = []
         for m in range(2):
-            flipped = sb.tile([P, HALF], F32, name="flipped%d" % m, align_bytes=64)
-            shrinks.append(sb.tile([P, 2], F32, name="shrink%d" % m))
-            nc.vector.tensor_scalar(flipped[:], scores[m, 1][:], -1.0, negs[m][:, 0:1], ALU.mult, ALU.min, accum_out=negs[m][:, 1:2])
-            nc.scalar.activation(shrinks[m][:], negs[m][:], ACT.Exp, bias=negs[m][:, 1:2], scale=-1.0)
-            nc.scalar.activation(probs[m][:, HALF:], flipped[:], ACT.Exp, bias=negs[m][:, 1:2], scale=-1.0, accum_out=sums[m][:, 1:2])
-        def inverse_total(m):
+            minus_scores = sb.tile([P, HALF], F32, name="minus_scores%d" % m, align_bytes=64)
+            shrink.append(sb.tile([P, 2], F32, name="shrink%d" % m))
+            nc.vector.tensor_scalar(minus_scores[:], scores[m, 1][:], -1.0, minus_max[m][:, 0:1], ALU.mult, ALU.min, accum_out=minus_max[m][:, 1:2])
+            nc.scalar.activation(shrink[m][:], minus_max[m][:], ACT.Exp, bias=minus_max[m][:, 1:2], scale=-1.0)
+            nc.scalar.activation(probs[m][:, HALF:], minus_scores[:], ACT.Exp, bias=minus_max[m][:, 1:2], scale=-1.0, accum_out=half_sums[m][:, 1:2])
+
+        def scale_over_row_sum(m):
             terms = sb.tile([P, 2], F32, name="terms%d" % m)
             total = sb.tile([P, 1], F32, name="total%d" % m)
-            inv = sb.tile([P, 1], F32, name="inv%d" % m)
-            nc.vector.scalar_tensor_tensor(terms[:], sums[m][:], 1.0 / 512.0, shrinks[m][:], ALU.mult, ALU.mult, accum_out=total[:])
-            nc.vector.reciprocal(inv[:], total[:])
-            return inv
+            inverse = sb.tile([P, 1], F32, name="inverse%d" % m)
+            nc.vector.scalar_tensor_tensor(terms[:], half_sums[m][:], 1.0 / OUT_SCALE, shrink[m][:], ALU.mult, ALU.mult, accum_out=total[:])
+            nc.vector.reciprocal(inverse[:], total[:])
+            return inverse
 
-        def store(m, h, y):
-            nc.sync.dma_start(out[m * P : (m + 1) * P, h * HALF : (h + 1) * HALF], y[:])
+        def store(m, h):
+            nc.sync.dma_start(out[m * P : (m + 1) * P, h * HALF : (h + 1) * HALF], y[m, h][:])
 
-        ys = {(m, h): sb.tile([P, HALF], F32, name="y%d_%d" % (m, h), align_bytes=64) for m in range(2) for h in range(2)}
-        inv = inverse_total(0)
-        factor = sb.tile([P, 1], F32, name="factor")
-        nc.vector.tensor_tensor(factor[:], inv[:], shrinks[0][:, 0:1], ALU.mult)
-        nc.vector.tensor_scalar(ys[0, 1][:], probs[0][:, HALF:], inv[:], None, ALU.mult)
-        store(0, 1, ys[0, 1])
-        nc.scalar.activation(ys[0, 0][:], probs[0][:, :HALF], ACT.Copy, scale=factor[:])
-        store(0, 0, ys[0, 0])
-        inv = inverse_total(1)
-        nc.vector.tensor_scalar(ys[1, 0][:], probs[1][:, :HALF], inv[:], shrinks[1][:, 0:1], ALU.mult, ALU.mult)
-        store(1, 0, ys[1, 0])
-        nc.vector.tensor_scalar(ys[1, 1][:], probs[1][:, HALF:], inv[:], None, ALU.mult)
-        store(1, 1, ys[1, 1])
+        y = {(m, h): sb.tile([P, HALF], F32, name="y%d_%d" % (m, h), align_bytes=64) for m in range(2) for h in range(2)}
+        inverse = scale_over_row_sum(0)
+        first_half_factor = sb.tile([P, 1], F32, name="first_half_factor")
+        nc.vector.tensor_tensor(first_half_factor[:], inverse[:], shrink[0][:, 0:1], ALU.mult)
+        nc.vector.tensor_scalar(y[0, 1][:], probs[0][:, HALF:], inverse[:], None, ALU.mult)
+        store(0, 1)
+        nc.scalar.activation(y[0, 0][:], probs[0][:, :HALF], ACT.Copy, scale=first_half_factor[:])
+        store(0, 0)
+        inverse = scale_over_row_sum(1)
+        nc.vector.tensor_scalar(y[1, 0][:], probs[1][:, :HALF], inverse[:], shrink[1][:, 0:1], ALU.mult, ALU.mult)
+        store(1, 0)
+        nc.vector.tensor_scalar(y[1, 1][:], probs[1][:, HALF:], inverse[:], None, ALU.mult)
+        store(1, 1)

from contextlib import ExitStack

import concourse.mybir as mybir
from concourse.masks import make_identity

D, T, I, U, V, Q = 512, 1024, 256, 512, 1024, 256
FLOPS = 2 * D * Q * T
BYTES = 4 * (3 * D * T + D * U + Q * T) + 4 * 128 * 16 * 2

F32 = mybir.dt.float32
BF16 = mybir.dt.bfloat16
U32 = mybir.dt.uint32
U16 = mybir.dt.uint16
U8 = mybir.dt.uint8
FP8X4 = mybir.dt.float8_e4m3fn_x4
ALU = mybir.AluOpType
ACT = mybir.ActivationFunctionType
AXIS = mybir.AxisListType

P = 128
PLANES = 4
QUARTERS = 4
QUARTER = T // QUARTERS
HALF = T // 2
OUT_SCALE = 512.0


def tile_attend_turnedkeys_kernel(tc, query, keys, cosn, sinn, kept, offs, offs2, offs3, offs4, out):
    nc = tc.nc
    with ExitStack() as ctx:
        lists = ctx.enter_context(tc.tile_pool(name="lists", bufs=1))
        sb = ctx.enter_context(tc.tile_pool(name="sb", bufs=1))
        ps = ctx.enter_context(tc.psum_pool(name="ps", bufs=1))

        def load_list(src, name):
            tile = lists.tile([P, I // 16], U16, name=name)
            nc.sync.dma_start(tile[:], src)
            return tile

        def load_plane(src, j, name):
            tile = sb.tile([P, src.shape[1]], F32, name=name, align_bytes=64)
            nc.sync.dma_start(tile[:], src.rearrange("(p j) c -> p j c", j=PLANES)[:, j, :])
            return tile[:]

        def load_pair(src, u, name):
            tile = sb.tile([P, 2, src.shape[1]], F32, name=name, align_bytes=64)
            nc.sync.dma_start(tile[:], src.rearrange("(p j) c -> p j c", j=PLANES)[:, 2 * u : 2 * u + 2, :])
            return tile[:, 0, :], tile[:, 1, :]

        key_plane, cos_plane, sin_plane, query_plane, kept_plane = {}, {}, {}, {}, {}
        cos_plane[0] = load_plane(cosn, 0, "cos0")
        distance_list = load_list(offs3, "distance_list")
        sin_plane[0] = load_plane(sinn, 0, "sin0")
        key_list = load_list(offs, "key_list")
        key_plane[0] = load_plane(keys, 0, "key0")
        key_plane[1] = load_plane(keys, 1, "key1")
        place_list = load_list(offs2, "place_list")
        kept_plane[0] = load_plane(kept, 0, "kept0")
        kept_plane[1] = load_plane(kept, 1, "kept1")
        cos_plane[1] = load_plane(cosn, 2, "cos1")
        sin_plane[1] = load_plane(sinn, 2, "sin1")
        key_plane[2], key_plane[3] = load_pair(keys, 1, "key23")
        kept_plane[2] = load_plane(kept, 2, "kept2")
        query_list = load_list(offs4, "query_list")
        query_plane[0] = load_plane(query, 0, "query0")
        kept_plane[3] = load_plane(kept, 3, "kept3")
        query_plane[1] = load_plane(query, 1, "query1")
        query_plane[2] = load_plane(query, 2, "query2")
        query_plane[3] = load_plane(query, 3, "query3")

        ident = sb.tile([P, P], F32, name="ident", align_bytes=64)
        make_identity(nc, ident[:])

        kf = [sb.tile([P, T], F32, name="kf%d" % j, align_bytes=64) for j in range(PLANES)]
        for j in range(PLANES):
            nc.gpsimd.memset(kf[j][:], 0.0)

        q_in = sb.tile([P, Q, PLANES], BF16, name="q_in", align_bytes=64)

        def gather_query_on_scalar(j):
            cast = sb.tile([P, V], BF16, name="query_bf16_%d" % j, align_bytes=64)
            nc.scalar.activation(cast[:], query_plane[j], ACT.Copy)
            nc.scalar.activation(q_in[:, :, j], cast[:].indirect(query_list[:]), ACT.Copy)

        def gather_query_on_vector(j):
            nc.vector.tensor_copy(q_in[:, :, j], query_plane[j].indirect(query_list[:]))

        def turn_and_place(u):
            even = sb.tile([P, I], F32, name="even%d" % u, align_bytes=64)
            odd = sb.tile([P, I], F32, name="odd%d" % u, align_bytes=64)
            cos_sin = sb.tile([P, 2, I], F32, name="cos_sin%d" % u, align_bytes=64)
            even_cos_sin = sb.tile([P, 2, I], F32, name="even_cos_sin%d" % u, align_bytes=64)
            odd_cos = sb.tile([P, I], F32, name="odd_cos%d" % u, align_bytes=64)
            minus_odd_sin = sb.tile([P, I], F32, name="minus_odd_sin%d" % u, align_bytes=64)
            nc.vector.tensor_copy(cos_sin[:, 0, :], cos_plane[u].indirect(distance_list[:]))
            nc.vector.tensor_copy(cos_sin[:, 1, :], sin_plane[u].indirect(distance_list[:]))
            nc.vector.tensor_copy(even[:], key_plane[2 * u].indirect(key_list[:]))
            nc.vector.tensor_copy(odd[:], key_plane[2 * u + 1].indirect(key_list[:]))
            nc.vector.tensor_tensor(even_cos_sin[:], cos_sin[:], even[:].unsqueeze(1).to_broadcast([P, 2, I]), ALU.mult)
            nc.vector.scalar_tensor_tensor(minus_odd_sin[:], odd[:], -1.0, cos_sin[:, 1, :], ALU.mult, ALU.mult)
            nc.vector.tensor_tensor(odd_cos[:], odd[:], cos_sin[:, 0, :], ALU.mult)
            nc.vector.tensor_tensor(kf[2 * u][:].indirect(place_list[:]), even_cos_sin[:, 0, :], minus_odd_sin[:], ALU.add)
            nc.vector.tensor_tensor(kf[2 * u + 1][:].indirect(place_list[:]), odd_cos[:], even_cos_sin[:, 1, :], ALU.add)

        def sum_banks(u):
            return [
                ps.tile([P, 2, 2, P], F32, name="sum%d_%d" % (u, g), tag="bank%d" % (QUARTERS * u + g))
                for g in range(QUARTERS)
            ]

        def add_transposed(banks, plane, e, start, stop):
            for g in range(QUARTERS):
                for b in range(2):
                    c0 = g * QUARTER + b * P
                    nc.tensor.matmul(banks[g][:, b, e, :], plane[:, c0 : c0 + P], ident[:], is_transpose=True,
                                     start=(start and b == 0), stop=(stop and b == 1))

        def sum_pair(banks, u):
            add_transposed(banks, kept_plane[2 * u], 0, True, False)
            add_transposed(banks, kept_plane[2 * u + 1], 1, False, False)
            add_transposed(banks, kf[2 * u], 0, False, False)
            add_transposed(banks, kf[2 * u + 1], 1, False, True)

        def round_pair(bank, u, g, copy):
            rounded = sb.tile([P, 2, P, 2], BF16, name="rounded%d_%d" % (u, g), align_bytes=64)
            copy(rounded[:], bank[:].rearrange("t b e p -> t b p e"))
            return rounded

        def turn_back(back, rounded, u):
            words = rounded[:].rearrange("t b p e -> t (b p e)").bitcast(F32)
            for b in range(2):
                nc.tensor.transpose(back[:, u, b * P : (b + 1) * P], words[:, b * P : (b + 1) * P], ident[:])

        turn_and_place(0)
        sums0 = sum_banks(0)
        sums1 = sum_banks(1)
        sum_pair(sums0, 0)
        backs = []
        for g in range(QUARTERS):
            rounded = round_pair(sums0[g], 0, g, nc.scalar.copy)
            back = ps.tile([P, 2, QUARTER], F32, name="back%d" % g, tag="bank%d" % g)
            turn_back(back, rounded, 0)
            backs.append(back)

        turn_and_place(1)
        gather_query_on_scalar(0)
        gather_query_on_scalar(1)
        sum_pair(sums1, 1)

        gather_query_on_vector(2)
        for g, copy in enumerate((nc.vector.tensor_copy, nc.scalar.copy, nc.scalar.copy)):
            turn_back(backs[g], round_pair(sums1[g], 1, g, copy), 1)
        gather_query_on_vector(3)
        turn_back(backs[3], round_pair(sums1[3], 1, 3, nc.vector.tensor_copy), 1)
        q_codes = sb.tile([P, Q], U32, name="q_codes", align_bytes=64)
        q_scales = sb.tile([P, Q], U8, name="q_scales", align_bytes=64)
        nc.vector.quantize_mx(q_codes[:].bitcast(FP8X4), q_scales[:], q_in[:].rearrange("p q j -> p (q j)"))

        scores = {}
        for h in range(2):
            for m in range(2):
                scores[m, h] = ps.tile([P, HALF], F32, name="score%d_%d" % (m, h), tag="bank%d" % (QUARTERS + 2 * h + m))

        k_in = []
        for g in range(QUARTERS):
            interleaved = sb.tile([P, QUARTER * PLANES], BF16, name="k_in%d" % g, align_bytes=64)
            nc.scalar.copy(interleaved[:].bitcast(F32).rearrange("p (t u) -> p t u", u=2), backs[g][:].rearrange("p u t -> p t u"))
            k_in.append(interleaved)
        for g in range(QUARTERS):
            k_codes = sb.tile([P, QUARTER], U32, name="k_codes%d" % g, align_bytes=64)
            k_scales = sb.tile([P, QUARTER], U8, name="k_scales%d" % g, align_bytes=64)
            nc.vector.quantize_mx(k_codes[:].bitcast(FP8X4), k_scales[:], k_in[g][:])
            cols = slice((g % 2) * QUARTER, (g % 2 + 1) * QUARTER)
            for m in range(2):
                rows = slice(m * P, (m + 1) * P)
                nc.tensor.matmul_mx(scores[m, g // 2][:, cols], lhsT=q_codes[:, rows].bitcast(FP8X4), lhsT_scale=q_scales[:, rows],
                                    rhs=k_codes[:].bitcast(FP8X4), rhs_scale=k_scales[:], start=True, stop=True)

        minus_max, half_sums, probs = [], [], []
        for m in range(2):
            minus_max.append(sb.tile([P, 2], F32, name="minus_max%d" % m))
            half_sums.append(sb.tile([P, 2], F32, name="half_sums%d" % m))
            probs.append(sb.tile([P, T], F32, name="probs%d" % m, align_bytes=64))
            nc.vector.tensor_reduce(minus_max[m][:, 0:1], scores[m, 0][:], AXIS.X, ALU.max, negate=True)
            nc.scalar.activation(probs[m][:, :HALF], scores[m, 0][:], ACT.Exp, bias=minus_max[m][:, 0:1], accum_out=half_sums[m][:, 0:1])
        shrink = []
        for m in range(2):
            minus_scores = sb.tile([P, HALF], F32, name="minus_scores%d" % m, align_bytes=64)
            shrink.append(sb.tile([P, 2], F32, name="shrink%d" % m))
            nc.vector.tensor_scalar(minus_scores[:], scores[m, 1][:], -1.0, minus_max[m][:, 0:1], ALU.mult, ALU.min, accum_out=minus_max[m][:, 1:2])
            nc.scalar.activation(shrink[m][:], minus_max[m][:], ACT.Exp, bias=minus_max[m][:, 1:2], scale=-1.0)
            nc.scalar.activation(probs[m][:, HALF:], minus_scores[:], ACT.Exp, bias=minus_max[m][:, 1:2], scale=-1.0, accum_out=half_sums[m][:, 1:2])

        def scale_over_row_sum(m):
            terms = sb.tile([P, 2], F32, name="terms%d" % m)
            total = sb.tile([P, 1], F32, name="total%d" % m)
            inverse = sb.tile([P, 1], F32, name="inverse%d" % m)
            nc.vector.scalar_tensor_tensor(terms[:], half_sums[m][:], 1.0 / OUT_SCALE, shrink[m][:], ALU.mult, ALU.mult, accum_out=total[:])
            nc.vector.reciprocal(inverse[:], total[:])
            return inverse

        def store(m, h):
            nc.sync.dma_start(out[m * P : (m + 1) * P, h * HALF : (h + 1) * HALF], y[m, h][:])

        y = {(m, h): sb.tile([P, HALF], F32, name="y%d_%d" % (m, h), align_bytes=64) for m in range(2) for h in range(2)}
        inverse = scale_over_row_sum(0)
        first_half_factor = sb.tile([P, 1], F32, name="first_half_factor")
        nc.vector.tensor_tensor(first_half_factor[:], inverse[:], shrink[0][:, 0:1], ALU.mult)
        nc.vector.tensor_scalar(y[0, 1][:], probs[0][:, HALF:], inverse[:], None, ALU.mult)
        store(0, 1)
        nc.scalar.activation(y[0, 0][:], probs[0][:, :HALF], ACT.Copy, scale=first_half_factor[:])
        store(0, 0)
        inverse = scale_over_row_sum(1)
        nc.vector.tensor_scalar(y[1, 0][:], probs[1][:, :HALF], inverse[:], shrink[1][:, 0:1], ALU.mult, ALU.mult)
        store(1, 0)
        nc.vector.tensor_scalar(y[1, 1][:], probs[1][:, HALF:], inverse[:], None, ALU.mult)
        store(1, 1)
